import numpy as np
import ml_dtypes


def mxq(x, axis, fmt="e4m3"):
    dtype, down = {"e4m3": (ml_dtypes.float8_e4m3fn, 7), "e5m2": (ml_dtypes.float8_e5m2, 14)}[fmt]
    v = np.moveaxis(np.asarray(x, np.float32).astype(ml_dtypes.bfloat16).astype(np.float64), axis, -1)
    blocks = v.reshape(v.shape[:-1] + (-1, 32))
    amax = np.abs(blocks).max(-1, keepdims=True)
    byte = np.maximum(np.where(amax > 0, np.frexp(amax)[1] - 1 + 127, 0) - down, 1)
    scale = np.exp2(byte - 127.0)
    codes = (blocks / scale).astype(np.float32).astype(dtype).astype(np.float64)
    return np.moveaxis((codes * scale).reshape(v.shape), -1, axis)


WIDE = False


def mx_kscale(k):
    if not WIDE:
        return np.ones(k)
    levels = np.array([30, -30])
    if k % 512:
        return np.exp2(np.random.permutation(np.resize(levels, k // 32))).repeat(32)
    a = np.empty((k // 512, 16))
    for p in range(k // 512):
        a[p, :8] = np.random.permutation(np.resize(levels, 8))
        for g in range(8):
            far = levels[np.abs(levels - a[p, g]) >= 10]
            a[p, g + 8] = far[np.random.randint(len(far))]
    return np.exp2(a.ravel()).repeat(32)


def f64(x):
    return np.asarray(x).astype(np.float64)


def striped(idx):
    return np.tile(np.asarray(idx).reshape(-1, 16).T, (8, 1)).astype(np.uint16)


def unstriped(offs):
    return offs[:16].T.reshape(-1).astype(np.int64)


E2M1 = np.array([0.0, 0.5, 1.0, 1.5, 2.0, 3.0, 4.0, 6.0, -0.0, -0.5, -1.0, -1.5, -2.0, -3.0, -4.0, -6.0])


def pack_weight(w, fmt):
    k, n = w.shape
    w = f64(np.asarray(w, np.float32).astype(ml_dtypes.bfloat16)).reshape(k // 32, 32, n)
    amax = np.abs(w).max(1)
    if fmt in ("e4m3", "e5m2"):
        byte = np.frexp(amax)[1] - 1 + 127 - (7 if fmt == "e4m3" else 14)
    else:
        mant, ex = np.frexp(amax / 6.0)
        byte = np.where(mant > 0.5, ex, ex - 1) + 127
    byte = np.clip(np.where(amax > 0, byte, 1), 1, 254)
    scaled = (w * np.exp2(127.0 - byte)[:, None, :]).reshape(k, n).astype(np.float32)
    by_word = np.ascontiguousarray(scaled.reshape(k // 512, 128, 4, n).transpose(0, 1, 3, 2))
    if fmt in ("e4m3", "e5m2"):
        words = by_word.astype(ml_dtypes.float8_e4m3fn if fmt == "e4m3" else ml_dtypes.float8_e5m2).view(np.uint8)
    else:
        c = by_word.astype(ml_dtypes.float4_e2m1fn).view(np.uint8) & 0xF
        words = (c[..., 0::2] | (c[..., 1::2] << 4)).reshape(k // 512, 128, 2 * n)
    return np.ascontiguousarray(words), np.ascontiguousarray(byte.astype(np.uint8).reshape(k // 512, 16, n))


def unpack_weight(words, scales, fmt):
    g, _, n = scales.shape
    words = np.ascontiguousarray(words).reshape(g, 128, n, -1)
    if fmt in ("e4m3", "e5m2"):
        vals = words.view(ml_dtypes.float8_e4m3fn if fmt == "e4m3" else ml_dtypes.float8_e5m2).astype(np.float64)
    else:
        nib = np.empty((g, 128, n, 4), np.uint8)
        nib[..., 0::2] = words & 0xF
        nib[..., 1::2] = words >> 4
        vals = E2M1[nib]
    vals = vals * np.repeat(np.exp2(scales.astype(np.float64) - 127.0), 8, axis=1)[..., None]
    return vals.transpose(0, 1, 3, 2).reshape(g * 512, n)


K, T, J, R, F, Z, N = 512, 512, 256, 512, 512, 1024, 256


def setup_inputs():
    n = np.random.standard_normal
    idx = np.random.permutation(T)[:J]
    idx2 = np.random.permutation(T)[:J]
    idx3 = np.random.permutation(Z)[:J]
    fk = mx_kscale(K)
    fr = mx_kscale(R)
    ff = mx_kscale(F)
    wp = pack_weight(n((K, R)) * 1 / np.sqrt(K) * fk[:, None] * fr, "e5m2")
    w2p = pack_weight(n((F, R)) * 1 / np.sqrt(F) * ff[:, None] * fr, "e4m3")
    wbp = pack_weight(n((R, N)) * 1 / np.sqrt(R) / fr[:, None], "e2m1")
    return {
        "xf": (n((K, T))).astype(np.float32),
        "fk": (np.random.uniform(0.5, 2.0, (K, 1)) / fk[:, None]).astype(np.float32),
        "w_words": wp[0],
        "w_scales": wp[1],
        "xo": (n((F, Z))).astype(np.float32),
        "fl": (np.random.uniform(0.5, 2.0, (F, 1)) / ff[:, None]).astype(np.float32),
        "so": (n((F, J)) * 0.8).astype(np.float32),
        "w2_words": w2p[0],
        "w2_scales": w2p[1],
        "wb_words": wbp[0],
        "wb_scales": wbp[1],
        "bi": (np.random.uniform(-0.5, 0.5, (1, N))).astype(np.float32),
        "offs": striped(idx),
        "offs2": striped(idx2),
        "offs3": striped(idx3),
    }


def reference(xf, fk, w_words, w_scales, xo, fl, so, w2_words, w2_scales, wb_words, wb_scales, bi, offs, offs2, offs3):
    idx = unstriped(offs)
    idx2 = unstriped(offs2)
    idx3 = unstriped(offs3)
    wu = unpack_weight(w_words, w_scales, "e5m2")
    w2u = unpack_weight(w2_words, w2_scales, "e4m3")
    wbu = unpack_weight(wb_words, wb_scales, "e2m1")
    u = (f64(xf)[:, idx] - f64(xf)[:, idx2]) * f64(fk)
    u2 = np.maximum(f64(xo)[:, idx3], f64(so)) * f64(fl)
    uq = mxq(u, 0, "e5m2")
    u2q = mxq(u2, 0, "e5m2")
    a = wu.T @ uq + w2u.T @ u2q
    ha = np.maximum(a, 0.0)
    h1 = np.pad(ha, ((0, 0), (2, 0)))[:, :J]
    hid = ha - 0.5 * h1
    hidq = mxq(hid, 0, "e5m2")
    p = hidq.T @ wbu
    ea = np.exp(0.7 * p + f64(bi))
    y = 256.0 * ea / np.sum(ea, axis=1, keepdims=True)
    return y

@@ -1,0 +1,248 @@
+from contextlib import ExitStack
+
+import concourse.mybir as mybir
+from concourse.masks import make_identity
+
+K, T, J, R, F, Z, N = 512, 512, 256, 512, 512, 1024, 256
+FLOPS = 2 * (K * R * J + F * R * J + R * J * N)
+
+F32 = mybir.dt.float32
+BF16 = mybir.dt.bfloat16
+I32 = mybir.dt.int32
+U32 = mybir.dt.uint32
+U16 = mybir.dt.uint16
+U8 = mybir.dt.uint8
+E5M2X4 = mybir.dt.float8_e5m2_x4
+E4M3X4 = mybir.dt.float8_e4m3fn_x4
+E2M1X4 = mybir.dt.float4_e2m1fn_x4
+ALU = mybir.AluOpType
+ACT = mybir.ActivationFunctionType
+AXIS = mybir.AxisListType
+
+P = 128
+PACK = 4
+HALF = 128
+HALVES = J // HALF
+LAG = 2
+
+
+def tile_list_sum_pickgaps_largest_lagged_rowshares_kernel(
+    tc, xf, fk, w_words, w_scales, xo, fl, so, w2_words, w2_scales, wb_words, wb_scales, bi, offs, offs2, offs3, out
+):
+    nc = tc.nc
+    with ExitStack() as ctx:
+        keep = ctx.enter_context(tc.tile_pool(name="keep", bufs=1))
+        psum = ctx.enter_context(tc.psum_pool(name="psum", bufs=1))
+
+        def sb(name, shape, dtype):
+            return keep.tile(shape, dtype, name=name, align_bytes=64)
+
+        list1 = sb("list1", [P, J // 16], U16)
+        list2 = sb("list2", [P, J // 16], U16)
+        list3 = sb("list3", [P, J // 16], U16)
+        xf_sb = [sb("xf%d" % t, [P, T], F32) for t in range(PACK)]
+        xo_sb = [sb("xo%d" % t, [P, Z], F32) for t in range(PACK)]
+        so_sb = sb("so_sb", [P, PACK, J], F32)
+        fk_sb = sb("fk_sb", [P, PACK], F32)
+        fl_sb = sb("fl_sb", [P, PACK], F32)
+        w_raw = sb("w_raw", [P, R], U32)
+        w2_raw = sb("w2_raw", [P, R], U32)
+        ws_raw = sb("ws_raw", [P, R], U8)
+        w2s_raw = sb("w2s_raw", [P, R], U8)
+        wb_sb = sb("wb_sb", [P, 2 * N], U8)
+        wbs_sb = sb("wbs_sb", [P, N], U8)
+        bi_col = sb("bi_col", [P, 2], F32)
+        ident = sb("ident", [P, P], F32)
+        ha = sb("ha", [P, (LAG + J) * PACK], F32)
+
+        nc.vector.memset(ws_raw[:].bitcast(I32), 0)
+        nc.vector.memset(w2s_raw[:].bitcast(I32), 0)
+        nc.vector.memset(wbs_sb[:].bitcast(I32), 0)
+        nc.vector.memset(ha[:, 0 : LAG * PACK], 0.0)
+
+        xf_planes = xf.rearrange("(p t) c -> p t c", t=PACK)
+        xo_planes = xo.rearrange("(p t) c -> p t c", t=PACK)
+
+        def load_scale_rows(queue, dst, src, q):
+            queue.dma_start(out=dst[32 * q : 32 * q + 4, :].bitcast(I32), in_=src[0, 4 * q : 4 * q + 4, :].bitcast(I32))
+
+        def words(src):
+            return src[0].rearrange("p n t -> p (n t)").bitcast(I32)
+
+        sync = nc.sync
+        sync.dma_start(out=list2[:], in_=offs2)
+        sync.dma_start(out=xf_sb[0][:], in_=xf_planes[:, 0, :])
+        sync.dma_start(out=list1[:], in_=offs)
+        sync.dma_start(out=xf_sb[1][:], in_=xf_planes[:, 1, :])
+        sync.dma_start(out=xf_sb[2][:], in_=xf_planes[:, 2, :])
+        sync.dma_start(out=fk_sb[:], in_=fk.rearrange("(p t) o -> p (t o)", t=PACK))
+        sync.dma_start(out=xf_sb[3][:], in_=xf_planes[:, 3, :])
+        sync.dma_start(out=so_sb[:], in_=so.rearrange("(p t) c -> p t c", t=PACK))
+        sync.dma_start(out=list3[:], in_=offs3)
+        sync.dma_start(out=xo_sb[0][:], in_=xo_planes[:, 0, :])
+        load_scale_rows(sync, ws_raw, w_scales, 0)
+        load_scale_rows(sync, ws_raw, w_scales, 1)
+        sync.dma_start(out=w_raw[:].bitcast(I32), in_=words(w_words))
+        load_scale_rows(sync, ws_raw, w_scales, 2)
+        load_scale_rows(sync, ws_raw, w_scales, 3)
+        sync.dma_start(out=xo_sb[1][:], in_=xo_planes[:, 1, :])
+        load_scale_rows(sync, w2s_raw, w2_scales, 0)
+        load_scale_rows(sync, w2s_raw, w2_scales, 1)
+        sync.dma_start(out=xo_sb[2][:], in_=xo_planes[:, 2, :])
+        load_scale_rows(sync, w2s_raw, w2_scales, 2)
+        load_scale_rows(sync, w2s_raw, w2_scales, 3)
+        sync.dma_start(out=xo_sb[3][:], in_=xo_planes[:, 3, :])
+        sync.dma_start(out=w2_raw[:].bitcast(I32), in_=words(w2_words))
+        sync.dma_start(out=wb_sb[:].bitcast(I32), in_=wb_words[0].bitcast(I32))
+
+        make_identity(nc, ident[:])
+        nc.gpsimd.dma_start(out=fl_sb[:], in_=fl.rearrange("(p t) o -> p (t o)", t=PACK))
+        nc.gpsimd.dma_start(out=bi_col[:], in_=bi.rearrange("o (p c) -> p (o c)", c=2))
+        for q in range(4):
+            load_scale_rows(nc.gpsimd, wbs_sb, wb_scales, q)
+
+        bias_ps = psum.tile([P, 2, P], F32, name="bias_ps")
+        for c in range(2):
+            nc.tensor.transpose(bias_ps[:, c, :], bi_col[:, c : c + 1].to_broadcast([P, P]), ident[:])
+        bias = sb("bias", [P, N], F32)
+        nc.scalar.copy(out=bias[:].rearrange("q (p c) -> q p c", c=2), in_=bias_ps[:].rearrange("q c p -> q p c"))
+
+        def interleave(dst, src):
+            nc.vector.tensor_copy(
+                out=dst.rearrange("p (c i t) -> p c t i", i=4, t=PACK),
+                in_=src.rearrange("p t (c i) -> p c t i", i=4),
+            )
+
+        def deal_words(dst, src):
+            nc.scalar.copy(
+                out=dst.rearrange("p (t c i) -> p c t i", t=PACK, i=4),
+                in_=src.rearrange("p (c i t) -> p c t i", t=PACK, i=4),
+            )
+
+        def deal_bytes(dst, src):
+            nc.vector.tensor_copy(
+                out=dst.rearrange("p (t m) -> p t m", t=PACK), in_=src.rearrange("p (m t) -> p t m", t=PACK)
+            )
+
+        second = sb("second", [P, PACK, J], F32)
+        gap = sb("gap", [P, PACK, J], F32)
+        u = sb("u", [P, PACK, J], F32)
+        for t in range(PACK):
+            nc.scalar.activation(out=second[:, t, :], in_=xf_sb[t][:].indirect(list2[:]), func=ACT.Copy)
+            nc.vector.tensor_tensor(
+                out=gap[:, t, :], in0=xf_sb[t][:].indirect(list1[:]), in1=second[:, t, :], op=ALU.subtract
+            )
+        for t in range(PACK):
+            nc.scalar.activation(out=u[:, t, :], in_=gap[:, t, :], func=ACT.Copy, scale=fk_sb[:, t : t + 1])
+        u_bf = sb("u_bf", [P, J * PACK], BF16)
+        interleave(u_bf[:], u[:])
+        u_codes = sb("u_codes", [P, J], U32)
+        u_scales = sb("u_scales", [P, J], U8)
+        nc.vector.quantize_mx(out=u_codes[:].bitcast(E5M2X4), scales=u_scales[:], in_=u_bf[:])
+
+        w_sb = sb("w_sb", [P, R], U32)
+        deal_words(w_sb[:], w_raw[:])
+
+        ws_sb = sb("ws_sb", [P, R], U8)
+        deal_bytes(ws_sb[:], ws_raw[:])
+
+        acc = [psum.tile([P, PACK, HALF], F32, name="acc%d" % h) for h in range(HALVES)]
+        for h in range(HALVES):
+            cols = slice(h * HALF, (h + 1) * HALF)
+            for t in range(PACK):
+                nc.tensor.matmul_mx(
+                    out=acc[h][:, t, :],
+                    lhsT=w_sb[:, t * P : (t + 1) * P].bitcast(E5M2X4),
+                    lhsT_scale=ws_sb[:, t * P : (t + 1) * P],
+                    rhs=u_codes[:, cols].bitcast(E5M2X4),
+                    rhs_scale=u_scales[:, cols],
+                    start=(t == 0),
+                    stop=False,
+                )
+
+        picked = sb("picked", [P, PACK, J], F32)
+        larger = sb("larger", [P, PACK, J], F32)
+        u2 = sb("u2", [P, PACK, J], F32)
+
+        def side_values(t, lo, hi):
+            entries = list3[:, lo // 16 : hi // 16]
+            nc.scalar.activation(out=picked[:, t, lo:hi], in_=xo_sb[t][:].indirect(entries), func=ACT.Copy)
+            nc.vector.tensor_tensor(
+                out=larger[:, t, lo:hi], in0=picked[:, t, lo:hi], in1=so_sb[:, t, lo:hi], op=ALU.max
+            )
+            nc.vector.tensor_scalar(
+                out=u2[:, t, lo:hi], in0=larger[:, t, lo:hi], scalar1=fl_sb[:, t : t + 1], scalar2=None, op0=ALU.mult
+            )
+
+        for t in range(PACK - 1):
+            side_values(t, 0, J)
+        w2s_sb = sb("w2s_sb", [P, R], U8)
+        deal_bytes(w2s_sb[:], w2s_raw[:])
+
+        w2_sb = sb("w2_sb", [P, R], U32)
+        u2_codes, u2_scales = [], []
+        for h in range(HALVES):
+            side_values(PACK - 1, h * HALF, (h + 1) * HALF)
+            u2_bf = sb("u2_bf%d" % h, [P, HALF * PACK], BF16)
+            interleave(u2_bf[:], u2[:, :, h * HALF : (h + 1) * HALF])
+            u2_codes.append(sb("u2_codes%d" % h, [P, HALF], U32))
+            u2_scales.append(sb("u2_scales%d" % h, [P, HALF], U8))
+            nc.vector.quantize_mx(out=u2_codes[h][:].bitcast(E5M2X4), scales=u2_scales[h][:], in_=u2_bf[:])
+        deal_words(w2_sb[:], w2_raw[:])
+        for h in range(HALVES):
+            for t in range(PACK):
+                nc.tensor.matmul_mx(
+                    out=acc[h][:, t, :],
+                    lhsT=w2_sb[:, t * P : (t + 1) * P].bitcast(E4M3X4),
+                    lhsT_scale=w2s_sb[:, t * P : (t + 1) * P],
+                    rhs=u2_codes[h][:].bitcast(E5M2X4),
+                    rhs_scale=u2_scales[h][:],
+                    start=False,
+                    stop=(t == PACK - 1),
+                )
+
+        width = HALF * PACK
+        logits = []
+        for h in range(HALVES):
+            now = ha[:, LAG * PACK + h * width : LAG * PACK + (h + 1) * width]
+            before = ha[:, h * width : (h + 1) * width]
+            nc.scalar.activation(
+                out=now.rearrange("p (j t) -> p j t", t=PACK), in_=acc[h][:].rearrange("p t j -> p j t"), func=ACT.Relu
+            )
+            hid_bf = sb("hid_bf%d" % h, [P, width], BF16)
+            nc.vector.scalar_tensor_tensor(
+                out=hid_bf[:], in0=before, scalar=-0.5, in1=now, op0=ALU.mult, op1=ALU.add
+            )
+            hid_codes = sb("hid_codes%d" % h, [P, HALF], U32)
+            hid_scales = sb("hid_scales%d" % h, [P, HALF], U8)
+            nc.vector.quantize_mx(out=hid_codes[:].bitcast(E5M2X4), scales=hid_scales[:], in_=hid_bf[:])
+            logits.append(psum.tile([P, N], F32, name="logits%d" % h))
+            nc.tensor.matmul_mx(
+                out=logits[h][:],
+                lhsT=hid_codes[:].bitcast(E5M2X4),
+                lhsT_scale=hid_scales[:],
+                rhs=wb_sb[:].bitcast(E2M1X4),
+                rhs_scale=wbs_sb[:],
+                start=True,
+                stop=True,
+            )
+
+        for h in range(HALVES):
+            neg = sb("neg%d" % h, [P, N], F32)
+            nc.vector.scalar_tensor_tensor(
+                out=neg[:], in0=logits[h][:], scalar=-0.7, in1=bias[:], op0=ALU.mult, op1=ALU.subtract
+            )
+            least = sb("least%d" % h, [P, 1], F32)
+            nc.vector.tensor_reduce(out=least[:], in_=neg[:], axis=AXIS.X, op=ALU.min)
+            ea = sb("ea%d" % h, [P, N], F32)
+            total = sb("total%d" % h, [P, 1], F32)
+            nc.scalar.activation(
+                out=ea[:], in_=neg[:], func=ACT.Exp, bias=least[:], scale=-1.0, accum_out=total[:]
+            )
+            inv = sb("inv%d" % h, [P, 1], F32)
+            nc.vector.reciprocal(out=inv[:], in_=total[:])
+            y = sb("y%d" % h, [P, N], F32)
+            nc.vector.tensor_scalar(
+                out=y[:], in0=ea[:], scalar1=inv[:], scalar2=256.0, op0=ALU.mult, op1=ALU.mult
+            )
+            nc.sync.dma_start(out=out[h * HALF : (h + 1) * HALF, :], in_=y[:])

@@ -60,6 +60,9 @@ def tile_list_sum_pickgaps_largest_lagged_rowshares_kernel(
         nc.vector.memset(wbs_sb[:].bitcast(I32), 0)
         nc.vector.memset(ha[:, 0 : LAG * PACK], 0.0)
 
+        warm = sb("warm", [P, 1], F32)
+        nc.scalar.activation(out=warm[:], in_=ha[:, 0:1], func=ACT.Exp)
+
         xf_planes = xf.rearrange("(p t) c -> p t c", t=PACK)
         xo_planes = xo.rearrange("(p t) c -> p t c", t=PACK)
 

@@ -34,30 +34,30 @@ def tile_list_sum_pickgaps_largest_lagged_rowshares_kernel(
         keep = ctx.enter_context(tc.tile_pool(name="keep", bufs=1))
         psum = ctx.enter_context(tc.psum_pool(name="psum", bufs=1))
 
-        def sb(name, shape, dtype):
-            return keep.tile(shape, dtype, name=name, align_bytes=64)
+        def sb(name, shape, dtype, tag=None):
+            return keep.tile(shape, dtype, name=name, tag=tag or name, align_bytes=64)
 
         list1 = sb("list1", [P, J // 16], U16)
         list2 = sb("list2", [P, J // 16], U16)
         list3 = sb("list3", [P, J // 16], U16)
         xf_sb = [sb("xf%d" % t, [P, T], F32) for t in range(PACK)]
         xo_sb = [sb("xo%d" % t, [P, Z], F32) for t in range(PACK)]
-        so_sb = sb("so_sb", [P, PACK, J], F32)
+        so_first = sb("so_first", [P, PACK - 1, J], F32)
+        so_last = sb("so_last", [P, J], F32)
         fk_sb = sb("fk_sb", [P, PACK], F32)
         fl_sb = sb("fl_sb", [P, PACK], F32)
         w_raw = sb("w_raw", [P, R], U32)
         w2_raw = sb("w2_raw", [P, R], U32)
-        ws_raw = sb("ws_raw", [P, R], U8)
-        w2s_raw = sb("w2s_raw", [P, R], U8)
+        scale_rows = sb("scale_rows", [P, 2 * R + N], U8)
+        ws_raw = scale_rows[:, 0:R]
+        w2s_raw = scale_rows[:, R : 2 * R]
+        wbs_sb = scale_rows[:, 2 * R : 2 * R + N]
         wb_sb = sb("wb_sb", [P, 2 * N], U8)
-        wbs_sb = sb("wbs_sb", [P, N], U8)
         bi_col = sb("bi_col", [P, 2], F32)
         ident = sb("ident", [P, P], F32)
         ha = sb("ha", [P, (LAG + J) * PACK], F32)
 
-        nc.vector.memset(ws_raw[:].bitcast(I32), 0)
-        nc.vector.memset(w2s_raw[:].bitcast(I32), 0)
-        nc.vector.memset(wbs_sb[:].bitcast(I32), 0)
+        nc.gpsimd.memset(scale_rows[:].bitcast(I32), 0)
         nc.vector.memset(ha[:, 0 : LAG * PACK], 0.0)
 
         warm = sb("warm", [P, 1], F32)
@@ -65,6 +65,7 @@ def tile_list_sum_pickgaps_largest_lagged_rowshares_kernel(
 
         xf_planes = xf.rearrange("(p t) c -> p t c", t=PACK)
         xo_planes = xo.rearrange("(p t) c -> p t c", t=PACK)
+        so_planes = so.rearrange("(p t) c -> p t c", t=PACK)
 
         def load_scale_rows(queue, dst, src, q):
             queue.dma_start(out=dst[32 * q : 32 * q + 4, :].bitcast(I32), in_=src[0, 4 * q : 4 * q + 4, :].bitcast(I32))
@@ -78,10 +79,10 @@ def tile_list_sum_pickgaps_largest_lagged_rowshares_kernel(
         sync.dma_start(out=list1[:], in_=offs)
         sync.dma_start(out=xf_sb[1][:], in_=xf_planes[:, 1, :])
         sync.dma_start(out=xf_sb[2][:], in_=xf_planes[:, 2, :])
-        sync.dma_start(out=fk_sb[:], in_=fk.rearrange("(p t) o -> p (t o)", t=PACK))
         sync.dma_start(out=xf_sb[3][:], in_=xf_planes[:, 3, :])
-        sync.dma_start(out=so_sb[:], in_=so.rearrange("(p t) c -> p t c", t=PACK))
+        sync.dma_start(out=so_first[:], in_=so_planes[:, 0 : PACK - 1, :])
         sync.dma_start(out=list3[:], in_=offs3)
+        sync.dma_start(out=fk_sb[:], in_=fk.rearrange("(p t) o -> p (t o)", t=PACK))
         sync.dma_start(out=xo_sb[0][:], in_=xo_planes[:, 0, :])
         load_scale_rows(sync, ws_raw, w_scales, 0)
         load_scale_rows(sync, ws_raw, w_scales, 1)
@@ -95,20 +96,19 @@ def tile_list_sum_pickgaps_largest_lagged_rowshares_kernel(
         load_scale_rows(sync, w2s_raw, w2_scales, 2)
         load_scale_rows(sync, w2s_raw, w2_scales, 3)
         sync.dma_start(out=xo_sb[3][:], in_=xo_planes[:, 3, :])
+        sync.dma_start(out=so_last[:], in_=so_planes[:, PACK - 1, :])
         sync.dma_start(out=w2_raw[:].bitcast(I32), in_=words(w2_words))
         sync.dma_start(out=wb_sb[:].bitcast(I32), in_=wb_words[0].bitcast(I32))
 
         make_identity(nc, ident[:])
-        nc.gpsimd.dma_start(out=fl_sb[:], in_=fl.rearrange("(p t) o -> p (t o)", t=PACK))
         nc.gpsimd.dma_start(out=bi_col[:], in_=bi.rearrange("o (p c) -> p (o c)", c=2))
+        nc.gpsimd.dma_start(out=fl_sb[:], in_=fl.rearrange("(p t) o -> p (t o)", t=PACK))
         for q in range(4):
             load_scale_rows(nc.gpsimd, wbs_sb, wb_scales, q)
 
         bias_ps = psum.tile([P, 2, P], F32, name="bias_ps")
         for c in range(2):
             nc.tensor.transpose(bias_ps[:, c, :], bi_col[:, c : c + 1].to_broadcast([P, P]), ident[:])
-        bias = sb("bias", [P, N], F32)
-        nc.scalar.copy(out=bias[:].rearrange("q (p c) -> q p c", c=2), in_=bias_ps[:].rearrange("q c p -> q p c"))
 
         def interleave(dst, src):
             nc.vector.tensor_copy(
@@ -127,26 +127,40 @@ def tile_list_sum_pickgaps_largest_lagged_rowshares_kernel(
                 out=dst.rearrange("p (t m) -> p t m", t=PACK), in_=src.rearrange("p (m t) -> p t m", t=PACK)
             )
 
-        second = sb("second", [P, PACK, J], F32)
-        gap = sb("gap", [P, PACK, J], F32)
+        second = [sb("second%d" % t, [P, J], F32) for t in range(PACK)]
+        gap = [sb("gap%d" % t, [P, J], F32) for t in range(PACK)]
         u = sb("u", [P, PACK, J], F32)
         for t in range(PACK):
-            nc.scalar.activation(out=second[:, t, :], in_=xf_sb[t][:].indirect(list2[:]), func=ACT.Copy)
+            if t == 0:
+                mid = J // 32
+                nc.scalar.activation(
+                    out=second[t][:, 0:HALF], in_=xf_sb[t][:].indirect(list2[:, 0:mid]), func=ACT.Copy
+                )
+                nc.vector.tensor_copy(out=second[t][:, HALF:J], in_=xf_sb[t][:].indirect(list2[:, mid : 2 * mid]))
+            else:
+                nc.scalar.activation(out=second[t][:], in_=xf_sb[t][:].indirect(list2[:]), func=ACT.Copy)
             nc.vector.tensor_tensor(
-                out=gap[:, t, :], in0=xf_sb[t][:].indirect(list1[:]), in1=second[:, t, :], op=ALU.subtract
+                out=gap[t][:], in0=xf_sb[t][:].indirect(list1[:]), in1=second[t][:], op=ALU.subtract
             )
-        for t in range(PACK):
-            nc.scalar.activation(out=u[:, t, :], in_=gap[:, t, :], func=ACT.Copy, scale=fk_sb[:, t : t + 1])
+        for t in range(PACK - 1):
+            nc.scalar.activation(out=u[:, t, :], in_=gap[t][:], func=ACT.Copy, scale=fk_sb[:, t : t + 1])
+        nc.vector.tensor_scalar(
+            out=u[:, PACK - 1, :],
+            in0=gap[PACK - 1][:],
+            scalar1=fk_sb[:, PACK - 1 : PACK],
+            scalar2=None,
+            op0=ALU.mult,
+        )
         u_bf = sb("u_bf", [P, J * PACK], BF16)
         interleave(u_bf[:], u[:])
         u_codes = sb("u_codes", [P, J], U32)
         u_scales = sb("u_scales", [P, J], U8)
         nc.vector.quantize_mx(out=u_codes[:].bitcast(E5M2X4), scales=u_scales[:], in_=u_bf[:])
 
-        w_sb = sb("w_sb", [P, R], U32)
+        w_sb = sb("w_sb", [P, R], U32, tag="second3")
         deal_words(w_sb[:], w_raw[:])
 
-        ws_sb = sb("ws_sb", [P, R], U8)
+        ws_sb = sb("ws_sb", [P, R], U8, tag="u_bf")
         deal_bytes(ws_sb[:], ws_raw[:])
 
         acc = [psum.tile([P, PACK, HALF], F32, name="acc%d" % h) for h in range(HALVES)]
@@ -163,35 +177,44 @@ def tile_list_sum_pickgaps_largest_lagged_rowshares_kernel(
                     stop=False,
                 )
 
-        picked = sb("picked", [P, PACK, J], F32)
-        larger = sb("larger", [P, PACK, J], F32)
         u2 = sb("u2", [P, PACK, J], F32)
 
-        def side_values(t, lo, hi):
-            entries = list3[:, lo // 16 : hi // 16]
-            nc.scalar.activation(out=picked[:, t, lo:hi], in_=xo_sb[t][:].indirect(entries), func=ACT.Copy)
-            nc.vector.tensor_tensor(
-                out=larger[:, t, lo:hi], in0=picked[:, t, lo:hi], in1=so_sb[:, t, lo:hi], op=ALU.max
-            )
-            nc.vector.tensor_scalar(
-                out=u2[:, t, lo:hi], in0=larger[:, t, lo:hi], scalar1=fl_sb[:, t : t + 1], scalar2=None, op0=ALU.mult
-            )
-
         for t in range(PACK - 1):
-            side_values(t, 0, J)
-        w2s_sb = sb("w2s_sb", [P, R], U8)
+            picked = sb("picked%d" % t, [P, J], F32, tag="gap2" if t == 0 else None)
+            nc.scalar.activation(out=picked[:], in_=xo_sb[t][:].indirect(list3[:]), func=ACT.Copy)
+            larger = sb("larger%d" % t, [P, J], F32)
+            nc.vector.tensor_tensor(out=larger[:], in0=picked[:], in1=so_first[:, t, :], op=ALU.max)
+            nc.vector.tensor_scalar(
+                out=u2[:, t, :], in0=larger[:], scalar1=fl_sb[:, t : t + 1], scalar2=None, op0=ALU.mult
+            )
+        w2s_sb = sb("w2s_sb", [P, R], U8, tag="larger1")
         deal_bytes(w2s_sb[:], w2s_raw[:])
 
-        w2_sb = sb("w2_sb", [P, R], U32)
         u2_codes, u2_scales = [], []
         for h in range(HALVES):
-            side_values(PACK - 1, h * HALF, (h + 1) * HALF)
+            last = PACK - 1
+            cols = slice(h * HALF, (h + 1) * HALF)
+            picked_last = sb("picked_last%d" % h, [P, HALF], F32)
+            entries = list3[:, h * (HALF // 16) : (h + 1) * (HALF // 16)]
+            nc.scalar.activation(out=picked_last[:], in_=xo_sb[last][:].indirect(entries), func=ACT.Copy)
+            larger = sb("larger_last%d" % h, [P, HALF], F32)
+            nc.vector.tensor_tensor(out=larger[:], in0=picked_last[:], in1=so_last[:, cols], op=ALU.max)
+            nc.vector.tensor_scalar(
+                out=u2[:, last, cols],
+                in0=larger[:],
+                scalar1=fl_sb[:, last : last + 1],
+                scalar2=None,
+                op0=ALU.mult,
+            )
             u2_bf = sb("u2_bf%d" % h, [P, HALF * PACK], BF16)
             interleave(u2_bf[:], u2[:, :, h * HALF : (h + 1) * HALF])
             u2_codes.append(sb("u2_codes%d" % h, [P, HALF], U32))
             u2_scales.append(sb("u2_scales%d" % h, [P, HALF], U8))
             nc.vector.quantize_mx(out=u2_codes[h][:].bitcast(E5M2X4), scales=u2_scales[h][:], in_=u2_bf[:])
+        w2_sb = sb("w2_sb", [P, R], U32, tag="xo3")
         deal_words(w2_sb[:], w2_raw[:])
+        bias = sb("bias", [P, N], F32, tag="picked_last1")
+        nc.scalar.copy(out=bias[:].rearrange("q (p c) -> q p c", c=2), in_=bias_ps[:].rearrange("q c p -> q p c"))
         for h in range(HALVES):
             for t in range(PACK):
                 nc.tensor.matmul_mx(

from contextlib import ExitStack

import concourse.mybir as mybir
from concourse.masks import make_identity

K, T, J, R, F, Z, N = 512, 512, 256, 512, 512, 1024, 256
FLOPS = 2 * (K * R * J + F * R * J + R * J * N)

F32 = mybir.dt.float32
BF16 = mybir.dt.bfloat16
I32 = mybir.dt.int32
U32 = mybir.dt.uint32
U16 = mybir.dt.uint16
U8 = mybir.dt.uint8
E5M2X4 = mybir.dt.float8_e5m2_x4
E4M3X4 = mybir.dt.float8_e4m3fn_x4
E2M1X4 = mybir.dt.float4_e2m1fn_x4
ALU = mybir.AluOpType
ACT = mybir.ActivationFunctionType
AXIS = mybir.AxisListType

P = 128
PACK = 4
HALF = 128
HALVES = J // HALF
LAG = 2


def tile_list_sum_pickgaps_largest_lagged_rowshares_kernel(
    tc, xf, fk, w_words, w_scales, xo, fl, so, w2_words, w2_scales, wb_words, wb_scales, bi, offs, offs2, offs3, out
):
    nc = tc.nc
    with ExitStack() as ctx:
        keep = ctx.enter_context(tc.tile_pool(name="keep", bufs=1))
        psum = ctx.enter_context(tc.psum_pool(name="psum", bufs=1))

        def sb(name, shape, dtype, tag=None):
            return keep.tile(shape, dtype, name=name, tag=tag or name, align_bytes=64)

        list1 = sb("list1", [P, J // 16], U16)
        list2 = sb("list2", [P, J // 16], U16)
        list3 = sb("list3", [P, J // 16], U16)
        xf_sb = [sb("xf%d" % t, [P, T], F32) for t in range(PACK)]
        xo_sb = [sb("xo%d" % t, [P, Z], F32) for t in range(PACK)]
        so_first = sb("so_first", [P, PACK - 1, J], F32)
        so_last = sb("so_last", [P, J], F32)
        fk_sb = sb("fk_sb", [P, PACK], F32)
        fl_sb = sb("fl_sb", [P, PACK], F32)
        w_raw = sb("w_raw", [P, R], U32)
        w2_raw = sb("w2_raw", [P, R], U32)
        scale_rows = sb("scale_rows", [P, 2 * R + N], U8)
        ws_raw = scale_rows[:, 0:R]
        w2s_raw = scale_rows[:, R : 2 * R]
        wbs_sb = scale_rows[:, 2 * R : 2 * R + N]
        wb_sb = sb("wb_sb", [P, 2 * N], U8)
        bi_col = sb("bi_col", [P, 2], F32)
        ident = sb("ident", [P, P], F32)
        ha = sb("ha", [P, (LAG + J) * PACK], F32)

        nc.gpsimd.memset(scale_rows[:].bitcast(I32), 0)
        nc.vector.memset(ha[:, 0 : LAG * PACK], 0.0)

        warm = sb("warm", [P, 1], F32)
        nc.scalar.activation(out=warm[:], in_=ha[:, 0:1], func=ACT.Exp)

        xf_planes = xf.rearrange("(p t) c -> p t c", t=PACK)
        xo_planes = xo.rearrange("(p t) c -> p t c", t=PACK)
        so_planes = so.rearrange("(p t) c -> p t c", t=PACK)

        def load_scale_rows(queue, dst, src, q):
            queue.dma_start(out=dst[32 * q : 32 * q + 4, :].bitcast(I32), in_=src[0, 4 * q : 4 * q + 4, :].bitcast(I32))

        def words(src):
            return src[0].rearrange("p n t -> p (n t)").bitcast(I32)

        sync = nc.sync
        sync.dma_start(out=list2[:], in_=offs2)
        sync.dma_start(out=xf_sb[0][:], in_=xf_planes[:, 0, :])
        sync.dma_start(out=list1[:], in_=offs)
        sync.dma_start(out=xf_sb[1][:], in_=xf_planes[:, 1, :])
        sync.dma_start(out=xf_sb[2][:], in_=xf_planes[:, 2, :])
        sync.dma_start(out=xf_sb[3][:], in_=xf_planes[:, 3, :])
        sync.dma_start(out=so_first[:], in_=so_planes[:, 0 : PACK - 1, :])
        sync.dma_start(out=list3[:], in_=offs3)
        sync.dma_start(out=fk_sb[:], in_=fk.rearrange("(p t) o -> p (t o)", t=PACK))
        sync.dma_start(out=xo_sb[0][:], in_=xo_planes[:, 0, :])
        load_scale_rows(sync, ws_raw, w_scales, 0)
        load_scale_rows(sync, ws_raw, w_scales, 1)
        sync.dma_start(out=w_raw[:].bitcast(I32), in_=words(w_words))
        load_scale_rows(sync, ws_raw, w_scales, 2)
        load_scale_rows(sync, ws_raw, w_scales, 3)
        sync.dma_start(out=xo_sb[1][:], in_=xo_planes[:, 1, :])
        load_scale_rows(sync, w2s_raw, w2_scales, 0)
        load_scale_rows(sync, w2s_raw, w2_scales, 1)
        sync.dma_start(out=xo_sb[2][:], in_=xo_planes[:, 2, :])
        load_scale_rows(sync, w2s_raw, w2_scales, 2)
        load_scale_rows(sync, w2s_raw, w2_scales, 3)
        sync.dma_start(out=xo_sb[3][:], in_=xo_planes[:, 3, :])
        sync.dma_start(out=so_last[:], in_=so_planes[:, PACK - 1, :])
        sync.dma_start(out=w2_raw[:].bitcast(I32), in_=words(w2_words))
        sync.dma_start(out=wb_sb[:].bitcast(I32), in_=wb_words[0].bitcast(I32))

        make_identity(nc, ident[:])
        nc.gpsimd.dma_start(out=bi_col[:], in_=bi.rearrange("o (p c) -> p (o c)", c=2))
        nc.gpsimd.dma_start(out=fl_sb[:], in_=fl.rearrange("(p t) o -> p (t o)", t=PACK))
        for q in range(4):
            load_scale_rows(nc.gpsimd, wbs_sb, wb_scales, q)

        bias_ps = psum.tile([P, 2, P], F32, name="bias_ps")
        for c in range(2):
            nc.tensor.transpose(bias_ps[:, c, :], bi_col[:, c : c + 1].to_broadcast([P, P]), ident[:])

        def interleave(dst, src):
            nc.vector.tensor_copy(
                out=dst.rearrange("p (c i t) -> p c t i", i=4, t=PACK),
                in_=src.rearrange("p t (c i) -> p c t i", i=4),
            )

        def deal_words(dst, src):
            nc.scalar.copy(
                out=dst.rearrange("p (t c i) -> p c t i", t=PACK, i=4),
                in_=src.rearrange("p (c i t) -> p c t i", t=PACK, i=4),
            )

        def deal_bytes(dst, src):
            nc.vector.tensor_copy(
                out=dst.rearrange("p (t m) -> p t m", t=PACK), in_=src.rearrange("p (m t) -> p t m", t=PACK)
            )

        second = [sb("second%d" % t, [P, J], F32) for t in range(PACK)]
        gap = [sb("gap%d" % t, [P, J], F32) for t in range(PACK)]
        u = sb("u", [P, PACK, J], F32)
        for t in range(PACK):
            if t == 0:
                mid = J // 32
                nc.scalar.activation(
                    out=second[t][:, 0:HALF], in_=xf_sb[t][:].indirect(list2[:, 0:mid]), func=ACT.Copy
                )
                nc.vector.tensor_copy(out=second[t][:, HALF:J], in_=xf_sb[t][:].indirect(list2[:, mid : 2 * mid]))
            else:
                nc.scalar.activation(out=second[t][:], in_=xf_sb[t][:].indirect(list2[:]), func=ACT.Copy)
            nc.vector.tensor_tensor(
                out=gap[t][:], in0=xf_sb[t][:].indirect(list1[:]), in1=second[t][:], op=ALU.subtract
            )
        for t in range(PACK - 1):
            nc.scalar.activation(out=u[:, t, :], in_=gap[t][:], func=ACT.Copy, scale=fk_sb[:, t : t + 1])
        nc.vector.tensor_scalar(
            out=u[:, PACK - 1, :],
            in0=gap[PACK - 1][:],
            scalar1=fk_sb[:, PACK - 1 : PACK],
            scalar2=None,
            op0=ALU.mult,
        )
        u_bf = sb("u_bf", [P, J * PACK], BF16)
        interleave(u_bf[:], u[:])
        u_codes = sb("u_codes", [P, J], U32)
        u_scales = sb("u_scales", [P, J], U8)
        nc.vector.quantize_mx(out=u_codes[:].bitcast(E5M2X4), scales=u_scales[:], in_=u_bf[:])

        w_sb = sb("w_sb", [P, R], U32, tag="second3")
        deal_words(w_sb[:], w_raw[:])

        ws_sb = sb("ws_sb", [P, R], U8, tag="u_bf")
        deal_bytes(ws_sb[:], ws_raw[:])

        acc = [psum.tile([P, PACK, HALF], F32, name="acc%d" % h) for h in range(HALVES)]
        for h in range(HALVES):
            cols = slice(h * HALF, (h + 1) * HALF)
            for t in range(PACK):
                nc.tensor.matmul_mx(
                    out=acc[h][:, t, :],
                    lhsT=w_sb[:, t * P : (t + 1) * P].bitcast(E5M2X4),
                    lhsT_scale=ws_sb[:, t * P : (t + 1) * P],
                    rhs=u_codes[:, cols].bitcast(E5M2X4),
                    rhs_scale=u_scales[:, cols],
                    start=(t == 0),
                    stop=False,
                )

        u2 = sb("u2", [P, PACK, J], F32)

        for t in range(PACK - 1):
            picked = sb("picked%d" % t, [P, J], F32, tag="gap2" if t == 0 else None)
            nc.scalar.activation(out=picked[:], in_=xo_sb[t][:].indirect(list3[:]), func=ACT.Copy)
            larger = sb("larger%d" % t, [P, J], F32)
            nc.vector.tensor_tensor(out=larger[:], in0=picked[:], in1=so_first[:, t, :], op=ALU.max)
            nc.vector.tensor_scalar(
                out=u2[:, t, :], in0=larger[:], scalar1=fl_sb[:, t : t + 1], scalar2=None, op0=ALU.mult
            )
        w2s_sb = sb("w2s_sb", [P, R], U8, tag="larger1")
        deal_bytes(w2s_sb[:], w2s_raw[:])

        u2_codes, u2_scales = [], []
        for h in range(HALVES):
            last = PACK - 1
            cols = slice(h * HALF, (h + 1) * HALF)
            picked_last = sb("picked_last%d" % h, [P, HALF], F32)
            entries = list3[:, h * (HALF // 16) : (h + 1) * (HALF // 16)]
            nc.scalar.activation(out=picked_last[:], in_=xo_sb[last][:].indirect(entries), func=ACT.Copy)
            larger = sb("larger_last%d" % h, [P, HALF], F32)
            nc.vector.tensor_tensor(out=larger[:], in0=picked_last[:], in1=so_last[:, cols], op=ALU.max)
            nc.vector.tensor_scalar(
                out=u2[:, last, cols],
                in0=larger[:],
                scalar1=fl_sb[:, last : last + 1],
                scalar2=None,
                op0=ALU.mult,
            )
            u2_bf = sb("u2_bf%d" % h, [P, HALF * PACK], BF16)
            interleave(u2_bf[:], u2[:, :, h * HALF : (h + 1) * HALF])
            u2_codes.append(sb("u2_codes%d" % h, [P, HALF], U32))
            u2_scales.append(sb("u2_scales%d" % h, [P, HALF], U8))
            nc.vector.quantize_mx(out=u2_codes[h][:].bitcast(E5M2X4), scales=u2_scales[h][:], in_=u2_bf[:])
        w2_sb = sb("w2_sb", [P, R], U32, tag="xo3")
        deal_words(w2_sb[:], w2_raw[:])
        bias = sb("bias", [P, N], F32, tag="picked_last1")
        nc.scalar.copy(out=bias[:].rearrange("q (p c) -> q p c", c=2), in_=bias_ps[:].rearrange("q c p -> q p c"))
        for h in range(HALVES):
            for t in range(PACK):
                nc.tensor.matmul_mx(
                    out=acc[h][:, t, :],
                    lhsT=w2_sb[:, t * P : (t + 1) * P].bitcast(E4M3X4),
                    lhsT_scale=w2s_sb[:, t * P : (t + 1) * P],
                    rhs=u2_codes[h][:].bitcast(E5M2X4),
                    rhs_scale=u2_scales[h][:],
                    start=False,
                    stop=(t == PACK - 1),
                )

        width = HALF * PACK
        logits = []
        for h in range(HALVES):
            now = ha[:, LAG * PACK + h * width : LAG * PACK + (h + 1) * width]
            before = ha[:, h * width : (h + 1) * width]
            nc.scalar.activation(
                out=now.rearrange("p (j t) -> p j t", t=PACK), in_=acc[h][:].rearrange("p t j -> p j t"), func=ACT.Relu
            )
            hid_bf = sb("hid_bf%d" % h, [P, width], BF16)
            nc.vector.scalar_tensor_tensor(
                out=hid_bf[:], in0=before, scalar=-0.5, in1=now, op0=ALU.mult, op1=ALU.add
            )
            hid_codes = sb("hid_codes%d" % h, [P, HALF], U32)
            hid_scales = sb("hid_scales%d" % h, [P, HALF], U8)
            nc.vector.quantize_mx(out=hid_codes[:].bitcast(E5M2X4), scales=hid_scales[:], in_=hid_bf[:])
            logits.append(psum.tile([P, N], F32, name="logits%d" % h))
            nc.tensor.matmul_mx(
                out=logits[h][:],
                lhsT=hid_codes[:].bitcast(E5M2X4),
                lhsT_scale=hid_scales[:],
                rhs=wb_sb[:].bitcast(E2M1X4),
                rhs_scale=wbs_sb[:],
                start=True,
                stop=True,
            )

        for h in range(HALVES):
            neg = sb("neg%d" % h, [P, N], F32)
            nc.vector.scalar_tensor_tensor(
                out=neg[:], in0=logits[h][:], scalar=-0.7, in1=bias[:], op0=ALU.mult, op1=ALU.subtract
            )
            least = sb("least%d" % h, [P, 1], F32)
            nc.vector.tensor_reduce(out=least[:], in_=neg[:], axis=AXIS.X, op=ALU.min)
            ea = sb("ea%d" % h, [P, N], F32)
            total = sb("total%d" % h, [P, 1], F32)
            nc.scalar.activation(
                out=ea[:], in_=neg[:], func=ACT.Exp, bias=least[:], scale=-1.0, accum_out=total[:]
            )
            inv = sb("inv%d" % h, [P, 1], F32)
            nc.vector.reciprocal(out=inv[:], in_=total[:])
            y = sb("y%d" % h, [P, N], F32)
            nc.vector.tensor_scalar(
                out=y[:], in0=ea[:], scalar1=inv[:], scalar2=256.0, op0=ALU.mult, op1=ALU.mult
            )
            nc.sync.dma_start(out=out[h * HALF : (h + 1) * HALF, :], in_=y[:])
